import numpy as np, ml_dtypes
CORES = [66,74,82,90,194,202,210,218]
N = 8
KB, QP = 1, 32
WB = 1
def setup_inputs(rng):
    q = rng.standard_normal((N, 128, QP), dtype=np.float32) / 4; k = rng.standard_normal((N, 128, KB * 128), dtype=np.float32)
    a = 2 * np.pi * rng.random((N, QP)); s = 400 * rng.random((N, QP)) ** 1.5; q[:, 0, :] = s * np.cos(a); q[:, 1, :] = s * np.sin(a); q[:, 2, :] = 150 * rng.standard_normal((N, QP)); k[:, 2, :] = 1 + k[:, 2, :] / 50
    a = (2 * np.pi * rng.random() + np.pi / 2 * (rng.permutation(N).reshape(N, 1, 1) + 0.5) / N - 0.5 + (np.arange(KB).reshape(1, KB, 1) + rng.random((N, KB, 128))) / KB).reshape(N, KB * 128); k[:, 0, :] = np.cos(a); k[:, 1, :] = np.sin(a)
    return {"q": q.astype(ml_dtypes.bfloat16), "k": k.astype(ml_dtypes.bfloat16), "v": rng.standard_normal((N, 128, KB * 128), dtype=np.float32).astype(ml_dtypes.bfloat16)}
def setup_inputs_big(rng):
    d = setup_inputs(rng)
    for k in ("v",): d[k] = (d[k].astype(np.float32) * 1048576.0).astype(d[k].dtype)
    return d
def setup_inputs_small(rng):
    d = setup_inputs(rng)
    for k in ("v",): d[k] = (d[k].astype(np.float32) * (1 / 1048576.0)).astype(d[k].dtype)
    return d
def reference(q, k, v):
    Q, K, V = q.astype(np.float64), k.astype(np.float64), v.astype(np.float64)
    y = np.zeros((N, QP, 128))
    for r in range(N):
        js = list(range(max(0, r - WB), r + 1))
        S = np.concatenate([K[j].T @ Q[r] for j in js], axis=0)
        P = np.exp(S - S.max(axis=0)); P = P / P.sum(axis=0)
        y[r] = P.T @ np.concatenate([V[j][:, 128 * b:128 * b + 128] for j in js for b in range(KB)], axis=0)
    return {"y": y.astype(ml_dtypes.bfloat16)}

@@ -1,0 +1,126 @@
+from concourse.mybir import AluOpType, AxisListType, ActivationFunctionType
+
+QP = 32
+KP = 128
+F = 128
+
+SCRATCH = {
+    "kv":    ("sbuf", [128, 256], "bfloat16"),
+    "kvp":   ("sbuf", [128, 256], "bfloat16"),
+    "qs":    ("sbuf", [128, QP], "bfloat16"),
+    "ones":  ("sbuf", [128, QP], "bfloat16"),
+    "ident": ("sbuf", [128, QP], "bfloat16"),
+    "st":    ("sbuf", [128, 8], "float32"),
+    "po":    ("sbuf", [128, KP], "bfloat16"),
+    "pp":    ("sbuf", [128, KP], "bfloat16"),
+    "pto":   ("sbuf", [128, QP], "bfloat16"),
+    "ptp":   ("sbuf", [128, QP], "bfloat16"),
+    "oo":    ("sbuf", [128, F], "bfloat16"),
+    "da":    ("sbuf", [128, QP], "bfloat16"),
+    "ysb":   ("sbuf", [128, F], "bfloat16"),
+    "psa":   ("psum", [128, 512], "float32"),
+    "psb":   ("psum", [128, 512], "float32"),
+    "psto":  ("psum", [128, 1024], "bfloat16"),
+    "pstp":  ("psum", [128, 1024], "bfloat16"),
+    "psoo":  ("psum", [128, 512], "float32"),
+    "pso":   ("psum", [128, 512], "float32"),
+}
+SEMAPHORES = ["ld", "ldq", "sent", "arr", "stored",
+              "e_ones", "e_id", "e_sto", "e_nmo", "e_po", "e_mo", "e_to", "e_pto", "e_oo", "e_oos",
+              "e_stp", "e_nm", "e_a", "e_pp", "e_da", "e_tp", "e_ptp", "e_l", "e_rl", "e_o", "e_y"]
+
+
+def rank_program(g, core, T, topo):
+    rank = T.rank_of(core)
+    if rank is None:
+        return
+    n = len(T.cores)
+    S = T.sem
+    pe, dve, act, sync = g.tensor, g.vector, g.scalar, g.sync
+    Exp, Copy = ActivationFunctionType.Exp, ActivationFunctionType.Copy
+    mult, add, amax = AluOpType.mult, AluOpType.add, AluOpType.max
+    Q = slice(0, QP)
+    col = lambda j: T.st[Q, j:j + 1]
+    NMO, LO, NM, LP, A, L, RL = range(7)
+    has_prev, has_next = rank > 0, rank < n - 1
+
+    sync.dma_start(T.kv[:, 0:KP], T.k[:, :]).then_inc(S.ld, 16)
+    act.dma_start(T.kv[:, KP:KP + F], T.v[:, :]).then_inc(S.ld, 16)
+    sync.dma_start(T.qs[:, :], T.q[:, :]).then_inc(S.ldq, 16)
+
+    dve.memset(T.ones[Q, :], 1.0).then_inc(S.e_ones, 1)
+    g.wait_ge(S.e_ones, 1)
+    g.affine_select(T.ident[Q, :], T.ones[Q, :], [[-1, QP]], AluOpType.is_equal, 0.0, 0, 1).then_inc(S.e_id, 1)
+
+    if has_next:
+        dst = T.cores[rank + 1]
+        rid, pid = topo.addr(dst, core)
+        mask = topo.mask(core, dst)
+        g.wait_ge(S.ld, 32)
+        g.remote_dma(T.kvp[:, :], T.kv[:, :], S.arr, S.sent, pid, rid, mask)
+    if has_prev:
+        src = T.cores[rank - 1]
+        arrive = bin(topo.mask(src, core)).count("1")
+
+    pe.wait_ge(S.ld, 32)
+    pe.wait_ge(S.ldq, 16)
+    pe.matmul(T.psa[Q, 0:KP], T.qs[:, :], T.kv[:, 0:KP], True, True).then_inc(S.e_sto, 1)
+    dve.wait_ge(S.e_sto, 1)
+    dve.tensor_reduce(col(NMO), T.psa[Q, 0:KP], AxisListType.X, amax, negate=True).then_inc(S.e_nmo, 1)
+    act.wait_ge(S.e_nmo, 1)
+    act.activation(T.po[Q, :], T.psa[Q, 0:KP], Exp, bias=col(NMO), scale=1.0, accum_out=col(LO)).then_inc(S.e_po, 1)
+    if has_prev:
+        dve.wait_ge(S.e_nmo, 1)
+        dve.tensor_scalar(T.psb[Q, KP:KP + 1], col(NMO), -1.0, None, mult).then_inc(S.e_mo, 1)
+    pe.wait_ge(S.e_po, 1)
+    pe.wait_ge(S.e_id, 1)
+    pe.transpose(T.psto[:, 0:QP], T.po[Q, :], T.ident[Q, :]).then_inc(S.e_to, 1)
+    dve.wait_ge(S.e_to, 1)
+    dve.tensor_copy(T.pto[:, :], T.psto[:, 0:QP]).then_inc(S.e_pto, 1)
+    pe.wait_ge(S.e_pto, 1)
+    pe.matmul(T.psoo[Q, 0:F], T.pto[:, :], T.kv[:, KP:KP + F], True, True).then_inc(S.e_oo, 1)
+
+    if not has_prev:
+        dve.wait_ge(S.e_po, 1)
+        dve.reciprocal(col(RL), col(LO)).then_inc(S.e_rl, 1)
+        dve.wait_ge(S.e_rl, 1)
+        dve.wait_ge(S.e_oo, 1)
+        dve.tensor_scalar(T.ysb[Q, :], T.psoo[Q, 0:F], col(RL), None, mult).then_inc(S.e_y, 1)
+    else:
+        dve.wait_ge(S.e_oo, 1)
+        dve.tensor_copy(T.oo[Q, :], T.psoo[Q, 0:F]).then_inc(S.e_oos, 1)
+
+        pe.wait_ge(S.e_mo, 1)
+        pe.wait_ge(S.arr, arrive)
+        pe.matmul(T.psb[Q, 0:KP], T.qs[:, :], T.kvp[:, 0:KP], True, True).then_inc(S.e_stp, 1)
+        dve.wait_ge(S.e_stp, 1)
+        dve.tensor_reduce(col(NM), T.psb[Q, 0:KP + 1], AxisListType.X, amax, negate=True).then_inc(S.e_nm, 1)
+        act.wait_ge(S.e_nm, 1)
+        act.activation(col(A), col(NMO), Exp, bias=col(NM), scale=-1.0).then_inc(S.e_a, 1)
+        act.activation(T.pp[Q, :], T.psb[Q, 0:KP], Exp, bias=col(NM), scale=1.0, accum_out=col(LP)).then_inc(S.e_pp, 1)
+        dve.wait_ge(S.e_a, 1)
+        dve.wait_ge(S.e_id, 1)
+        dve.tensor_scalar(T.da[Q, :], T.ident[Q, :], col(A), None, mult).then_inc(S.e_da, 1)
+        pe.wait_ge(S.e_da, 1)
+        pe.wait_ge(S.e_oos, 1)
+        pe.matmul(T.pso[Q, 0:F], T.da[Q, :], T.oo[Q, :], True, False)
+        pe.wait_ge(S.e_pp, 1)
+        pe.transpose(T.pstp[:, 0:QP], T.pp[Q, :], T.ident[Q, :]).then_inc(S.e_tp, 1)
+        act.wait_ge(S.e_tp, 1)
+        act.activation(T.ptp[:, :], T.pstp[:, 0:QP], Copy).then_inc(S.e_ptp, 1)
+        dve.wait_ge(S.e_po, 1)
+        dve.wait_ge(S.e_pp, 1)
+        dve.tensor_scalar(col(L), col(A), col(LO), col(LP), mult, add).then_inc(S.e_l, 1)
+        dve.wait_ge(S.e_l, 1)
+        dve.reciprocal(col(RL), col(L)).then_inc(S.e_rl, 1)
+        pe.wait_ge(S.e_ptp, 1)
+        pe.matmul(T.pso[Q, 0:F], T.ptp[:, :], T.kvp[:, KP:KP + F], False, True).then_inc(S.e_o, 1)
+        dve.wait_ge(S.e_rl, 1)
+        dve.wait_ge(S.e_o, 1)
+        dve.tensor_scalar(T.ysb[Q, :], T.pso[Q, 0:F], col(RL), None, mult).then_inc(S.e_y, 1)
+
+    sync.wait_ge(S.e_y, 1)
+    sync.dma_start(T.y[:, :], T.ysb[Q, :]).then_inc(S.stored, 16)
+    sync.wait_ge(S.stored, 16)
+    if has_next:
+        g.wait_ge(S.sent, bin(mask).count("1"))

@@ -5,8 +5,10 @@ KP = 128
 F = 128
 
 SCRATCH = {
-    "kv":    ("sbuf", [128, 256], "bfloat16"),
-    "kvp":   ("sbuf", [128, 256], "bfloat16"),
+    "ks":    ("sbuf", [128, KP], "bfloat16"),
+    "vs":    ("sbuf", [128, F], "bfloat16"),
+    "kp":    ("sbuf", [128, KP], "bfloat16"),
+    "vp":    ("sbuf", [128, F], "bfloat16"),
     "qs":    ("sbuf", [128, QP], "bfloat16"),
     "ones":  ("sbuf", [128, QP], "bfloat16"),
     "ident": ("sbuf", [128, QP], "bfloat16"),
@@ -15,18 +17,16 @@ SCRATCH = {
     "pp":    ("sbuf", [128, KP], "bfloat16"),
     "pto":   ("sbuf", [128, QP], "bfloat16"),
     "ptp":   ("sbuf", [128, QP], "bfloat16"),
-    "oo":    ("sbuf", [128, F], "bfloat16"),
     "da":    ("sbuf", [128, QP], "bfloat16"),
     "ysb":   ("sbuf", [128, F], "bfloat16"),
     "psa":   ("psum", [128, 512], "float32"),
     "psb":   ("psum", [128, 512], "float32"),
-    "psto":  ("psum", [128, 1024], "bfloat16"),
+    "psto":  ("psum", [128, 512], "float32"),
     "pstp":  ("psum", [128, 1024], "bfloat16"),
-    "psoo":  ("psum", [128, 512], "float32"),
     "pso":   ("psum", [128, 512], "float32"),
 }
-SEMAPHORES = ["ld", "ldq", "sent", "arr", "stored",
-              "e_ones", "e_id", "e_sto", "e_nmo", "e_po", "e_mo", "e_to", "e_pto", "e_oo", "e_oos",
+SEMAPHORES = ["ldk", "ldv", "ldq", "sent", "arrk", "arrv", "stored",
+              "e_ones", "e_id", "e_sto", "e_nmo", "e_po", "e_mo", "e_to", "e_pto",
               "e_stp", "e_nm", "e_a", "e_pp", "e_da", "e_tp", "e_ptp", "e_l", "e_rl", "e_o", "e_y"]
 
 
@@ -44,9 +44,9 @@ def rank_program(g, core, T, topo):
     NMO, LO, NM, LP, A, L, RL = range(7)
     has_prev, has_next = rank > 0, rank < n - 1
 
-    sync.dma_start(T.kv[:, 0:KP], T.k[:, :]).then_inc(S.ld, 16)
-    act.dma_start(T.kv[:, KP:KP + F], T.v[:, :]).then_inc(S.ld, 16)
-    sync.dma_start(T.qs[:, :], T.q[:, :]).then_inc(S.ldq, 16)
+    sync.dma_start(T.ks[:, :], T.k[:, :]).then_inc(S.ldk, 16)
+    act.dma_start(T.qs[:, :], T.q[:, :]).then_inc(S.ldq, 16)
+    sync.dma_start(T.vs[:, :], T.v[:, :]).then_inc(S.ldv, 16)
 
     dve.memset(T.ones[Q, :], 1.0).then_inc(S.e_ones, 1)
     g.wait_ge(S.e_ones, 1)
@@ -56,43 +56,40 @@ def rank_program(g, core, T, topo):
         dst = T.cores[rank + 1]
         rid, pid = topo.addr(dst, core)
         mask = topo.mask(core, dst)
-        g.wait_ge(S.ld, 32)
-        g.remote_dma(T.kvp[:, :], T.kv[:, :], S.arr, S.sent, pid, rid, mask)
+        g.wait_ge(S.ldk, 16)
+        g.remote_dma(T.kp[:, :], T.ks[:, :], S.arrk, S.sent, pid, rid, mask)
+        g.wait_ge(S.ldv, 16)
+        g.remote_dma(T.vp[:, :], T.vs[:, :], S.arrv, S.sent, pid, rid, mask)
     if has_prev:
         src = T.cores[rank - 1]
         arrive = bin(topo.mask(src, core)).count("1")
 
-    pe.wait_ge(S.ld, 32)
+    pe.wait_ge(S.ldk, 16)
     pe.wait_ge(S.ldq, 16)
-    pe.matmul(T.psa[Q, 0:KP], T.qs[:, :], T.kv[:, 0:KP], True, True).then_inc(S.e_sto, 1)
+    pe.matmul(T.psa[Q, 0:KP], T.qs[:, :], T.ks[:, :], True, True).then_inc(S.e_sto, 1)
     dve.wait_ge(S.e_sto, 1)
     dve.tensor_reduce(col(NMO), T.psa[Q, 0:KP], AxisListType.X, amax, negate=True).then_inc(S.e_nmo, 1)
     act.wait_ge(S.e_nmo, 1)
     act.activation(T.po[Q, :], T.psa[Q, 0:KP], Exp, bias=col(NMO), scale=1.0, accum_out=col(LO)).then_inc(S.e_po, 1)
-    if has_prev:
-        dve.wait_ge(S.e_nmo, 1)
-        dve.tensor_scalar(T.psb[Q, KP:KP + 1], col(NMO), -1.0, None, mult).then_inc(S.e_mo, 1)
-    pe.wait_ge(S.e_po, 1)
-    pe.wait_ge(S.e_id, 1)
-    pe.transpose(T.psto[:, 0:QP], T.po[Q, :], T.ident[Q, :]).then_inc(S.e_to, 1)
-    dve.wait_ge(S.e_to, 1)
-    dve.tensor_copy(T.pto[:, :], T.psto[:, 0:QP]).then_inc(S.e_pto, 1)
-    pe.wait_ge(S.e_pto, 1)
-    pe.matmul(T.psoo[Q, 0:F], T.pto[:, :], T.kv[:, KP:KP + F], True, True).then_inc(S.e_oo, 1)
 
     if not has_prev:
+        pe.wait_ge(S.e_po, 1)
+        pe.wait_ge(S.e_id, 1)
+        pe.matmul(T.psto[:, 0:QP], T.po[Q, :], T.ident[Q, :], True, True).then_inc(S.e_to, 1)
+        act.wait_ge(S.e_to, 1)
+        act.activation(T.pto[:, :], T.psto[:, 0:QP], Copy).then_inc(S.e_pto, 1)
         dve.wait_ge(S.e_po, 1)
         dve.reciprocal(col(RL), col(LO)).then_inc(S.e_rl, 1)
-        dve.wait_ge(S.e_rl, 1)
-        dve.wait_ge(S.e_oo, 1)
-        dve.tensor_scalar(T.ysb[Q, :], T.psoo[Q, 0:F], col(RL), None, mult).then_inc(S.e_y, 1)
+        pe.wait_ge(S.e_pto, 1)
+        pe.wait_ge(S.ldv, 16)
+        pe.matmul(T.pso[Q, 0:F], T.pto[:, :], T.vs[:, :], True, True).then_inc(S.e_o, 1)
     else:
-        dve.wait_ge(S.e_oo, 1)
-        dve.tensor_copy(T.oo[Q, :], T.psoo[Q, 0:F]).then_inc(S.e_oos, 1)
+        dve.wait_ge(S.e_nmo, 1)
+        dve.tensor_scalar(T.psb[Q, KP:KP + 1], col(NMO), -1.0, None, mult).then_inc(S.e_mo, 1)
 
         pe.wait_ge(S.e_mo, 1)
-        pe.wait_ge(S.arr, arrive)
-        pe.matmul(T.psb[Q, 0:KP], T.qs[:, :], T.kvp[:, 0:KP], True, True).then_inc(S.e_stp, 1)
+        pe.wait_ge(S.arrk, arrive)
+        pe.matmul(T.psb[Q, 0:KP], T.qs[:, :], T.kp[:, :], True, True).then_inc(S.e_stp, 1)
         dve.wait_ge(S.e_stp, 1)
         dve.tensor_reduce(col(NM), T.psb[Q, 0:KP + 1], AxisListType.X, amax, negate=True).then_inc(S.e_nm, 1)
         act.wait_ge(S.e_nm, 1)
@@ -102,10 +99,13 @@ def rank_program(g, core, T, topo):
         dve.wait_ge(S.e_id, 1)
         dve.tensor_scalar(T.da[Q, :], T.ident[Q, :], col(A), None, mult).then_inc(S.e_da, 1)
         pe.wait_ge(S.e_da, 1)
-        pe.wait_ge(S.e_oos, 1)
-        pe.matmul(T.pso[Q, 0:F], T.da[Q, :], T.oo[Q, :], True, False)
+        pe.wait_ge(S.e_po, 1)
+        pe.matmul(T.psto[:, 0:QP], T.po[Q, :], T.da[Q, :], True, True).then_inc(S.e_to, 1)
         pe.wait_ge(S.e_pp, 1)
+        pe.wait_ge(S.e_id, 1)
         pe.transpose(T.pstp[:, 0:QP], T.pp[Q, :], T.ident[Q, :]).then_inc(S.e_tp, 1)
+        act.wait_ge(S.e_to, 1)
+        act.activation(T.pto[:, :], T.psto[:, 0:QP], Copy).then_inc(S.e_pto, 1)
         act.wait_ge(S.e_tp, 1)
         act.activation(T.ptp[:, :], T.pstp[:, 0:QP], Copy).then_inc(S.e_ptp, 1)
         dve.wait_ge(S.e_po, 1)
@@ -113,14 +113,19 @@ def rank_program(g, core, T, topo):
         dve.tensor_scalar(col(L), col(A), col(LO), col(LP), mult, add).then_inc(S.e_l, 1)
         dve.wait_ge(S.e_l, 1)
         dve.reciprocal(col(RL), col(L)).then_inc(S.e_rl, 1)
+        pe.wait_ge(S.e_pto, 1)
+        pe.wait_ge(S.ldv, 16)
+        pe.matmul(T.pso[Q, 0:F], T.pto[:, :], T.vs[:, :], True, False)
         pe.wait_ge(S.e_ptp, 1)
-        pe.matmul(T.pso[Q, 0:F], T.ptp[:, :], T.kvp[:, KP:KP + F], False, True).then_inc(S.e_o, 1)
-        dve.wait_ge(S.e_rl, 1)
-        dve.wait_ge(S.e_o, 1)
-        dve.tensor_scalar(T.ysb[Q, :], T.pso[Q, 0:F], col(RL), None, mult).then_inc(S.e_y, 1)
+        pe.wait_ge(S.arrv, arrive)
+        pe.matmul(T.pso[Q, 0:F], T.ptp[:, :], T.vp[:, :], False, True).then_inc(S.e_o, 1)
+
+    dve.wait_ge(S.e_rl, 1)
+    dve.wait_ge(S.e_o, 1)
+    dve.tensor_scalar(T.ysb[Q, :], T.pso[Q, 0:F], col(RL), None, mult).then_inc(S.e_y, 1)
 
     sync.wait_ge(S.e_y, 1)
     sync.dma_start(T.y[:, :], T.ysb[Q, :]).then_inc(S.stored, 16)
     sync.wait_ge(S.stored, 16)
     if has_next:
-        g.wait_ge(S.sent, bin(mask).count("1"))
+        g.wait_ge(S.sent, 2 * bin(mask).count("1"))

@@ -3,31 +3,38 @@ from concourse.mybir import AluOpType, AxisListType, ActivationFunctionType
 QP = 32
 KP = 128
 F = 128
+H = F // 2
 
 SCRATCH = {
+    "kd":    ("dram", [128, KP], "bfloat16"),
     "ks":    ("sbuf", [128, KP], "bfloat16"),
     "vs":    ("sbuf", [128, F], "bfloat16"),
     "kp":    ("sbuf", [128, KP], "bfloat16"),
     "vp":    ("sbuf", [128, F], "bfloat16"),
     "qs":    ("sbuf", [128, QP], "bfloat16"),
-    "ones":  ("sbuf", [128, QP], "bfloat16"),
+    "dd":    ("sbuf", [128, QP], "float32"),
+    "sq":    ("sbuf", [128, QP], "float32"),
+    "nmask": ("sbuf", [128, QP], "float32"),
     "ident": ("sbuf", [128, QP], "bfloat16"),
     "st":    ("sbuf", [128, 8], "float32"),
     "po":    ("sbuf", [128, KP], "bfloat16"),
-    "pp":    ("sbuf", [128, KP], "bfloat16"),
+    "pp":    ("sbuf", [128, KP + 8], "bfloat16"),
     "pto":   ("sbuf", [128, QP], "bfloat16"),
     "ptp":   ("sbuf", [128, QP], "bfloat16"),
+    "oo":    ("sbuf", [128, F], "bfloat16"),
     "da":    ("sbuf", [128, QP], "bfloat16"),
     "ysb":   ("sbuf", [128, F], "bfloat16"),
     "psa":   ("psum", [128, 512], "float32"),
     "psb":   ("psum", [128, 512], "float32"),
-    "psto":  ("psum", [128, 512], "float32"),
+    "psto":  ("psum", [128, 1024], "bfloat16"),
     "pstp":  ("psum", [128, 1024], "bfloat16"),
-    "pso":   ("psum", [128, 512], "float32"),
+    "psoo":  ("psum", [128, 512], "float32"),
+    "pso1":  ("psum", [128, 512], "float32"),
+    "pso2":  ("psum", [128, 512], "float32"),
 }
-SEMAPHORES = ["ldk", "ldv", "ldq", "sent", "arrk", "arrv", "stored",
-              "e_ones", "e_id", "e_sto", "e_nmo", "e_po", "e_mo", "e_to", "e_pto",
-              "e_stp", "e_nm", "e_a", "e_pp", "e_da", "e_tp", "e_ptp", "e_l", "e_rl", "e_o", "e_y"]
+SEMAPHORES = ["ldkd", "ldk", "ldv", "ldq", "sent", "arrk", "arrv", "stored",
+              "e_d", "e_sq", "e_nk", "e_id", "e_sto", "e_nmo", "e_po", "e_mo", "e_lo1", "e_to", "e_pto", "e_oo", "e_oos",
+              "e_stp", "e_nm", "e_pp", "e_da", "e_tp", "e_ptp", "e_l", "e_rl", "e_o1", "e_o2", "e_y1", "e_y2"]
 
 
 def rank_program(g, core, T, topo):
@@ -37,27 +44,34 @@ def rank_program(g, core, T, topo):
     n = len(T.cores)
     S = T.sem
     pe, dve, act, sync = g.tensor, g.vector, g.scalar, g.sync
-    Exp, Copy = ActivationFunctionType.Exp, ActivationFunctionType.Copy
-    mult, add, amax = AluOpType.mult, AluOpType.add, AluOpType.max
+    Exp, Copy, Relu = ActivationFunctionType.Exp, ActivationFunctionType.Copy, ActivationFunctionType.Relu
+    mult, add, amax, amin = AluOpType.mult, AluOpType.add, AluOpType.max, AluOpType.min
     Q = slice(0, QP)
     col = lambda j: T.st[Q, j:j + 1]
-    NMO, LO, NM, LP, A, L, RL = range(7)
+    NMO, LO, LO1, NM, ACC, L, RL = range(7)
     has_prev, has_next = rank > 0, rank < n - 1
 
-    sync.dma_start(T.ks[:, :], T.k[:, :]).then_inc(S.ldk, 16)
+    if has_next:
+        sync.dma_start(T.kd[:, :], T.k[:, :]).then_inc(S.ldkd, 16)
     act.dma_start(T.qs[:, :], T.q[:, :]).then_inc(S.ldq, 16)
-    sync.dma_start(T.vs[:, :], T.v[:, :]).then_inc(S.ldv, 16)
+    sync.dma_start(T.ks[:, :], T.k[:, :]).then_inc(S.ldk, 16)
+    act.dma_start(T.vs[:, :], T.v[:, :]).then_inc(S.ldv, 16)
 
-    dve.memset(T.ones[Q, :], 1.0).then_inc(S.e_ones, 1)
-    g.wait_ge(S.e_ones, 1)
-    g.affine_select(T.ident[Q, :], T.ones[Q, :], [[-1, QP]], AluOpType.is_equal, 0.0, 0, 1).then_inc(S.e_id, 1)
+    g.iota(T.dd[Q, :], [[-1, QP]], 0, 1, allow_small_or_imprecise_dtypes=True).then_inc(S.e_d, 1)
+    dve.wait_ge(S.e_d, 1)
+    dve.tensor_tensor(T.sq[Q, :], T.dd[Q, :], T.dd[Q, :], mult).then_inc(S.e_sq, 1)
+    act.wait_ge(S.e_sq, 1)
+    act.activation(T.ident[Q, :], T.sq[Q, :], Exp, scale=-200.0).then_inc(S.e_id, 1)
+    if has_prev:
+        dve.wait_ge(S.e_sq, 1)
+        dve.tensor_scalar(T.nmask[Q, :], T.sq[Q, :], 1.0, -2.0, amin, mult).then_inc(S.e_nk, 1)
 
     if has_next:
         dst = T.cores[rank + 1]
         rid, pid = topo.addr(dst, core)
         mask = topo.mask(core, dst)
-        g.wait_ge(S.ldk, 16)
-        g.remote_dma(T.kp[:, :], T.ks[:, :], S.arrk, S.sent, pid, rid, mask)
+        g.wait_ge(S.ldkd, 16)
+        g.remote_dma(T.kp[:, :], T.kd[:, :], S.arrk, S.sent, pid, rid, mask)
         g.wait_ge(S.ldv, 16)
         g.remote_dma(T.vp[:, :], T.vs[:, :], S.arrv, S.sent, pid, rid, mask)
     if has_prev:
@@ -71,21 +85,30 @@ def rank_program(g, core, T, topo):
     dve.tensor_reduce(col(NMO), T.psa[Q, 0:KP], AxisListType.X, amax, negate=True).then_inc(S.e_nmo, 1)
     act.wait_ge(S.e_nmo, 1)
     act.activation(T.po[Q, :], T.psa[Q, 0:KP], Exp, bias=col(NMO), scale=1.0, accum_out=col(LO)).then_inc(S.e_po, 1)
-
-    if not has_prev:
-        pe.wait_ge(S.e_po, 1)
-        pe.wait_ge(S.e_id, 1)
-        pe.matmul(T.psto[:, 0:QP], T.po[Q, :], T.ident[Q, :], True, True).then_inc(S.e_to, 1)
-        act.wait_ge(S.e_to, 1)
-        act.activation(T.pto[:, :], T.psto[:, 0:QP], Copy).then_inc(S.e_pto, 1)
-        dve.wait_ge(S.e_po, 1)
-        dve.reciprocal(col(RL), col(LO)).then_inc(S.e_rl, 1)
-        pe.wait_ge(S.e_pto, 1)
-        pe.wait_ge(S.ldv, 16)
-        pe.matmul(T.pso[Q, 0:F], T.pto[:, :], T.vs[:, :], True, True).then_inc(S.e_o, 1)
-    else:
+    if has_prev:
         dve.wait_ge(S.e_nmo, 1)
         dve.tensor_scalar(T.psb[Q, KP:KP + 1], col(NMO), -1.0, None, mult).then_inc(S.e_mo, 1)
+    pe.wait_ge(S.e_po, 1)
+    pe.wait_ge(S.e_id, 1)
+    pe.transpose(T.psto[:, 0:QP], T.po[Q, :], T.ident[Q, :]).then_inc(S.e_to, 1)
+    act.wait_ge(S.e_to, 1)
+    act.activation(T.pto[:, :], T.psto[:, 0:QP], Copy).then_inc(S.e_pto, 1)
+    pe.wait_ge(S.e_pto, 1)
+    pe.wait_ge(S.ldv, 16)
+    pe.matmul(T.psoo[Q, 0:F], T.pto[:, :], T.vs[:, :], True, True).then_inc(S.e_oo, 1)
+
+    if not has_prev:
+        dve.wait_ge(S.e_po, 1)
+        dve.reciprocal(col(RL), col(LO)).then_inc(S.e_rl, 1)
+        dve.wait_ge(S.e_rl, 1)
+        dve.wait_ge(S.e_oo, 1)
+        dve.tensor_scalar(T.ysb[Q, :], T.psoo[Q, 0:F], col(RL), None, mult).then_inc(S.e_y1, 1)
+        sync.wait_ge(S.e_y1, 1)
+    else:
+        dve.wait_ge(S.e_po, 1)
+        dve.tensor_scalar(col(LO1), col(LO), -1.0, None, add).then_inc(S.e_lo1, 1)
+        dve.wait_ge(S.e_oo, 1)
+        dve.tensor_copy(T.oo[Q, :], T.psoo[Q, 0:F]).then_inc(S.e_oos, 1)
 
         pe.wait_ge(S.e_mo, 1)
         pe.wait_ge(S.arrk, arrive)
@@ -93,38 +116,41 @@ def rank_program(g, core, T, topo):
         dve.wait_ge(S.e_stp, 1)
         dve.tensor_reduce(col(NM), T.psb[Q, 0:KP + 1], AxisListType.X, amax, negate=True).then_inc(S.e_nm, 1)
         act.wait_ge(S.e_nm, 1)
-        act.activation(col(A), col(NMO), Exp, bias=col(NM), scale=-1.0).then_inc(S.e_a, 1)
-        act.activation(T.pp[Q, :], T.psb[Q, 0:KP], Exp, bias=col(NM), scale=1.0, accum_out=col(LP)).then_inc(S.e_pp, 1)
-        dve.wait_ge(S.e_a, 1)
-        dve.wait_ge(S.e_id, 1)
-        dve.tensor_scalar(T.da[Q, :], T.ident[Q, :], col(A), None, mult).then_inc(S.e_da, 1)
-        pe.wait_ge(S.e_da, 1)
-        pe.wait_ge(S.e_po, 1)
-        pe.matmul(T.psto[:, 0:QP], T.po[Q, :], T.da[Q, :], True, True).then_inc(S.e_to, 1)
+        act.activation(T.pp[Q, 0:KP + 1], T.psb[Q, 0:KP + 1], Exp, bias=col(NM), scale=1.0,
+                       accum_out=col(ACC)).then_inc(S.e_pp, 1)
+        a = T.pp[Q, KP:KP + 1]
+
         pe.wait_ge(S.e_pp, 1)
-        pe.wait_ge(S.e_id, 1)
-        pe.transpose(T.pstp[:, 0:QP], T.pp[Q, :], T.ident[Q, :]).then_inc(S.e_tp, 1)
-        act.wait_ge(S.e_to, 1)
-        act.activation(T.pto[:, :], T.psto[:, 0:QP], Copy).then_inc(S.e_pto, 1)
+        pe.transpose(T.pstp[:, 0:QP], T.pp[Q, 0:KP], T.ident[Q, :]).then_inc(S.e_tp, 1)
+        act.wait_ge(S.e_pp, 1)
+        act.wait_ge(S.e_nk, 1)
+        act.activation(T.da[Q, :], T.nmask[Q, :], Relu, bias=a, scale=1.0).then_inc(S.e_da, 1)
         act.wait_ge(S.e_tp, 1)
         act.activation(T.ptp[:, :], T.pstp[:, 0:QP], Copy).then_inc(S.e_ptp, 1)
-        dve.wait_ge(S.e_po, 1)
         dve.wait_ge(S.e_pp, 1)
-        dve.tensor_scalar(col(L), col(A), col(LO), col(LP), mult, add).then_inc(S.e_l, 1)
+        dve.wait_ge(S.e_lo1, 1)
+        dve.tensor_scalar(col(L), a, col(LO1), col(ACC), mult, add).then_inc(S.e_l, 1)
         dve.wait_ge(S.e_l, 1)
         dve.reciprocal(col(RL), col(L)).then_inc(S.e_rl, 1)
-        pe.wait_ge(S.e_pto, 1)
-        pe.wait_ge(S.ldv, 16)
-        pe.matmul(T.pso[Q, 0:F], T.pto[:, :], T.vs[:, :], True, False)
+
+        pe.wait_ge(S.e_da, 1)
+        pe.wait_ge(S.e_oos, 1)
+        pe.matmul(T.pso1[Q, 0:H], T.da[Q, :], T.oo[Q, 0:H], True, False)
+        pe.matmul(T.pso2[Q, 0:H], T.da[Q, :], T.oo[Q, H:F], True, False)
         pe.wait_ge(S.e_ptp, 1)
         pe.wait_ge(S.arrv, arrive)
-        pe.matmul(T.pso[Q, 0:F], T.ptp[:, :], T.vp[:, :], False, True).then_inc(S.e_o, 1)
+        pe.matmul(T.pso1[Q, 0:H], T.ptp[:, :], T.vp[:, 0:H], False, True).then_inc(S.e_o1, 1)
+        pe.matmul(T.pso2[Q, 0:H], T.ptp[:, :], T.vp[:, H:F], False, True).then_inc(S.e_o2, 1)
 
-    dve.wait_ge(S.e_rl, 1)
-    dve.wait_ge(S.e_o, 1)
-    dve.tensor_scalar(T.ysb[Q, :], T.pso[Q, 0:F], col(RL), None, mult).then_inc(S.e_y, 1)
+        dve.wait_ge(S.e_rl, 1)
+        dve.wait_ge(S.e_o1, 1)
+        dve.tensor_scalar(T.ysb[Q, 0:H], T.pso1[Q, 0:H], col(RL), None, mult).then_inc(S.e_y1, 1)
+        act.wait_ge(S.e_rl, 1)
+        act.wait_ge(S.e_o2, 1)
+        act.activation(T.ysb[Q, H:F], T.pso2[Q, 0:H], Copy, scale=col(RL)).then_inc(S.e_y2, 1)
+        sync.wait_ge(S.e_y1, 1)
+        sync.wait_ge(S.e_y2, 1)
 
-    sync.wait_ge(S.e_y, 1)
     sync.dma_start(T.y[:, :], T.ysb[Q, :]).then_inc(S.stored, 16)
     sync.wait_ge(S.stored, 16)
     if has_next:

from concourse.mybir import AluOpType, AxisListType, ActivationFunctionType

QP = 32
KP = 128
F = 128
H = F // 2

SCRATCH = {
    "kd":    ("dram", [128, KP], "bfloat16"),
    "ks":    ("sbuf", [128, KP], "bfloat16"),
    "vs":    ("sbuf", [128, F], "bfloat16"),
    "kp":    ("sbuf", [128, KP], "bfloat16"),
    "vp":    ("sbuf", [128, F], "bfloat16"),
    "qs":    ("sbuf", [128, QP], "bfloat16"),
    "dd":    ("sbuf", [128, QP], "float32"),
    "sq":    ("sbuf", [128, QP], "float32"),
    "nmask": ("sbuf", [128, QP], "float32"),
    "ident": ("sbuf", [128, QP], "bfloat16"),
    "st":    ("sbuf", [128, 8], "float32"),
    "po":    ("sbuf", [128, KP], "bfloat16"),
    "pp":    ("sbuf", [128, KP + 8], "bfloat16"),
    "pto":   ("sbuf", [128, QP], "bfloat16"),
    "ptp":   ("sbuf", [128, QP], "bfloat16"),
    "oo":    ("sbuf", [128, F], "bfloat16"),
    "da":    ("sbuf", [128, QP], "bfloat16"),
    "ysb":   ("sbuf", [128, F], "bfloat16"),
    "psa":   ("psum", [128, 512], "float32"),
    "psb":   ("psum", [128, 512], "float32"),
    "psto":  ("psum", [128, 1024], "bfloat16"),
    "pstp":  ("psum", [128, 1024], "bfloat16"),
    "psoo":  ("psum", [128, 512], "float32"),
    "pso1":  ("psum", [128, 512], "float32"),
    "pso2":  ("psum", [128, 512], "float32"),
}
SEMAPHORES = ["ldkd", "ldk", "ldv", "ldq", "sent", "arrk", "arrv", "stored",
              "e_d", "e_sq", "e_nk", "e_id", "e_sto", "e_nmo", "e_po", "e_mo", "e_lo1", "e_to", "e_pto", "e_oo", "e_oos",
              "e_stp", "e_nm", "e_pp", "e_da", "e_tp", "e_ptp", "e_l", "e_rl", "e_o1", "e_o2", "e_y1", "e_y2"]


def rank_program(g, core, T, topo):
    rank = T.rank_of(core)
    if rank is None:
        return
    n = len(T.cores)
    S = T.sem
    pe, dve, act, sync = g.tensor, g.vector, g.scalar, g.sync
    Exp, Copy, Relu = ActivationFunctionType.Exp, ActivationFunctionType.Copy, ActivationFunctionType.Relu
    mult, add, amax, amin = AluOpType.mult, AluOpType.add, AluOpType.max, AluOpType.min
    Q = slice(0, QP)
    col = lambda j: T.st[Q, j:j + 1]
    NMO, LO, LO1, NM, ACC, L, RL = range(7)
    has_prev, has_next = rank > 0, rank < n - 1

    if has_next:
        sync.dma_start(T.kd[:, :], T.k[:, :]).then_inc(S.ldkd, 16)
    act.dma_start(T.qs[:, :], T.q[:, :]).then_inc(S.ldq, 16)
    sync.dma_start(T.ks[:, :], T.k[:, :]).then_inc(S.ldk, 16)
    act.dma_start(T.vs[:, :], T.v[:, :]).then_inc(S.ldv, 16)

    g.iota(T.dd[Q, :], [[-1, QP]], 0, 1, allow_small_or_imprecise_dtypes=True).then_inc(S.e_d, 1)
    dve.wait_ge(S.e_d, 1)
    dve.tensor_tensor(T.sq[Q, :], T.dd[Q, :], T.dd[Q, :], mult).then_inc(S.e_sq, 1)
    act.wait_ge(S.e_sq, 1)
    act.activation(T.ident[Q, :], T.sq[Q, :], Exp, scale=-200.0).then_inc(S.e_id, 1)
    if has_prev:
        dve.wait_ge(S.e_sq, 1)
        dve.tensor_scalar(T.nmask[Q, :], T.sq[Q, :], 1.0, -2.0, amin, mult).then_inc(S.e_nk, 1)

    if has_next:
        dst = T.cores[rank + 1]
        rid, pid = topo.addr(dst, core)
        mask = topo.mask(core, dst)
        g.wait_ge(S.ldkd, 16)
        g.remote_dma(T.kp[:, :], T.kd[:, :], S.arrk, S.sent, pid, rid, mask)
        g.wait_ge(S.ldv, 16)
        g.remote_dma(T.vp[:, :], T.vs[:, :], S.arrv, S.sent, pid, rid, mask)
    if has_prev:
        src = T.cores[rank - 1]
        arrive = bin(topo.mask(src, core)).count("1")

    pe.wait_ge(S.ldk, 16)
    pe.wait_ge(S.ldq, 16)
    pe.matmul(T.psa[Q, 0:KP], T.qs[:, :], T.ks[:, :], True, True).then_inc(S.e_sto, 1)
    dve.wait_ge(S.e_sto, 1)
    dve.tensor_reduce(col(NMO), T.psa[Q, 0:KP], AxisListType.X, amax, negate=True).then_inc(S.e_nmo, 1)
    act.wait_ge(S.e_nmo, 1)
    act.activation(T.po[Q, :], T.psa[Q, 0:KP], Exp, bias=col(NMO), scale=1.0, accum_out=col(LO)).then_inc(S.e_po, 1)
    if has_prev:
        dve.wait_ge(S.e_nmo, 1)
        dve.tensor_scalar(T.psb[Q, KP:KP + 1], col(NMO), -1.0, None, mult).then_inc(S.e_mo, 1)
    pe.wait_ge(S.e_po, 1)
    pe.wait_ge(S.e_id, 1)
    pe.transpose(T.psto[:, 0:QP], T.po[Q, :], T.ident[Q, :]).then_inc(S.e_to, 1)
    act.wait_ge(S.e_to, 1)
    act.activation(T.pto[:, :], T.psto[:, 0:QP], Copy).then_inc(S.e_pto, 1)
    pe.wait_ge(S.e_pto, 1)
    pe.wait_ge(S.ldv, 16)
    pe.matmul(T.psoo[Q, 0:F], T.pto[:, :], T.vs[:, :], True, True).then_inc(S.e_oo, 1)

    if not has_prev:
        dve.wait_ge(S.e_po, 1)
        dve.reciprocal(col(RL), col(LO)).then_inc(S.e_rl, 1)
        dve.wait_ge(S.e_rl, 1)
        dve.wait_ge(S.e_oo, 1)
        dve.tensor_scalar(T.ysb[Q, :], T.psoo[Q, 0:F], col(RL), None, mult).then_inc(S.e_y1, 1)
        sync.wait_ge(S.e_y1, 1)
    else:
        dve.wait_ge(S.e_po, 1)
        dve.tensor_scalar(col(LO1), col(LO), -1.0, None, add).then_inc(S.e_lo1, 1)
        dve.wait_ge(S.e_oo, 1)
        dve.tensor_copy(T.oo[Q, :], T.psoo[Q, 0:F]).then_inc(S.e_oos, 1)

        pe.wait_ge(S.e_mo, 1)
        pe.wait_ge(S.arrk, arrive)
        pe.matmul(T.psb[Q, 0:KP], T.qs[:, :], T.kp[:, :], True, True).then_inc(S.e_stp, 1)
        dve.wait_ge(S.e_stp, 1)
        dve.tensor_reduce(col(NM), T.psb[Q, 0:KP + 1], AxisListType.X, amax, negate=True).then_inc(S.e_nm, 1)
        act.wait_ge(S.e_nm, 1)
        act.activation(T.pp[Q, 0:KP + 1], T.psb[Q, 0:KP + 1], Exp, bias=col(NM), scale=1.0,
                       accum_out=col(ACC)).then_inc(S.e_pp, 1)
        a = T.pp[Q, KP:KP + 1]

        pe.wait_ge(S.e_pp, 1)
        pe.transpose(T.pstp[:, 0:QP], T.pp[Q, 0:KP], T.ident[Q, :]).then_inc(S.e_tp, 1)
        act.wait_ge(S.e_pp, 1)
        act.wait_ge(S.e_nk, 1)
        act.activation(T.da[Q, :], T.nmask[Q, :], Relu, bias=a, scale=1.0).then_inc(S.e_da, 1)
        act.wait_ge(S.e_tp, 1)
        act.activation(T.ptp[:, :], T.pstp[:, 0:QP], Copy).then_inc(S.e_ptp, 1)
        dve.wait_ge(S.e_pp, 1)
        dve.wait_ge(S.e_lo1, 1)
        dve.tensor_scalar(col(L), a, col(LO1), col(ACC), mult, add).then_inc(S.e_l, 1)
        dve.wait_ge(S.e_l, 1)
        dve.reciprocal(col(RL), col(L)).then_inc(S.e_rl, 1)

        pe.wait_ge(S.e_da, 1)
        pe.wait_ge(S.e_oos, 1)
        pe.matmul(T.pso1[Q, 0:H], T.da[Q, :], T.oo[Q, 0:H], True, False)
        pe.matmul(T.pso2[Q, 0:H], T.da[Q, :], T.oo[Q, H:F], True, False)
        pe.wait_ge(S.e_ptp, 1)
        pe.wait_ge(S.arrv, arrive)
        pe.matmul(T.pso1[Q, 0:H], T.ptp[:, :], T.vp[:, 0:H], False, True).then_inc(S.e_o1, 1)
        pe.matmul(T.pso2[Q, 0:H], T.ptp[:, :], T.vp[:, H:F], False, True).then_inc(S.e_o2, 1)

        dve.wait_ge(S.e_rl, 1)
        dve.wait_ge(S.e_o1, 1)
        dve.tensor_scalar(T.ysb[Q, 0:H], T.pso1[Q, 0:H], col(RL), None, mult).then_inc(S.e_y1, 1)
        act.wait_ge(S.e_rl, 1)
        act.wait_ge(S.e_o2, 1)
        act.activation(T.ysb[Q, H:F], T.pso2[Q, 0:H], Copy, scale=col(RL)).then_inc(S.e_y2, 1)
        sync.wait_ge(S.e_y1, 1)
        sync.wait_ge(S.e_y2, 1)

    sync.dma_start(T.y[:, :], T.ysb[Q, :]).then_inc(S.stored, 16)
    sync.wait_ge(S.stored, 16)
    if has_next:
        g.wait_ge(S.sent, 2 * bin(mask).count("1"))
